import numpy as np, ml_dtypes
CORES = [5,29,101,125,133,157,229,253]
N = 8
import mx_ref
BF = ml_dtypes.bfloat16
def entries(a):
    return np.ascontiguousarray(a.T).reshape(-1)
def table(e):
    return np.ascontiguousarray(np.reshape(e, (-1, 16)).T).astype(np.int32)
def cols(t, e):
    v = np.concatenate([t.reshape(128, -1, 4), np.zeros((128, 1, 4), BF)], axis=1)
    return np.ascontiguousarray(v[:, e]).reshape(128, -1)
def f(rng, *shape):
    return mx_ref.flush((rng.standard_normal(shape, dtype=np.float32) * np.exp2(rng.integers(-2, 3, shape[:-1] + (1,)))).astype(BF))
def wide(rng, *shape, cols=0):
    v = rng.standard_normal(shape, dtype=np.float32) * np.exp2(rng.integers(-12, 13, shape)).astype(np.float32)
    if cols: v *= np.repeat(np.exp2(rng.integers(-cols, cols + 1, shape[:-2] + (1, shape[-1] // 4))) * (rng.random(shape[:-2] + (1, shape[-1] // 4)) > 0.0625), 4, axis=-1).astype(np.float32)
    return mx_ref.flush(v.astype(BF))
T, W, UN, CR = 512, 512, 160, 80
HOST = [0 if k < 128 else 1 for k in CORES]
def lists(rng, full=False, alike=False):
    uni, need, pos = np.full((N, 2, UN), -1), np.full((N, N, CR), -1), []
    for q in range(N):
        for g in range(2):
            mates = [r for r in range(N) if HOST[r] == g]
            n = UN if full else int(rng.integers(CR >> 1, CR + 1)) if alike else int(rng.integers(UN >> 2, UN + 1))
            at = rng.permutation(UN)[:n]
            uni[q, g, at] = rng.permutation(T)[:n]
            who = rng.permutation(np.repeat(np.arange(len(mates)), CR))[:n]
            for i, r in enumerate(mates):
                e, others = at[who == i], at[who != i]
                if alike: e = at
                else:
                    k = CR if full else int(rng.integers(max(len(e), CR >> 2), min(CR, n) + 1))
                    e = np.concatenate([e, rng.permutation(others)[:k - len(e)]])
                need[r, q, rng.permutation(CR)[:len(e)]] = e
    for r in range(N):
        ok = np.flatnonzero(need[r].reshape(-1) >= 0)
        pos.append(table(rng.permutation(ok)[:W] if full else rng.choice(ok, W)))
    return {"uni": np.stack([table(e.reshape(-1)) for e in uni]), "need": np.stack([table(e.reshape(-1)) for e in need]), "pos": np.stack(pos)}
def setup_inputs(rng):
    return {"c": f(rng, N, 128, 4 * T), "w": f(rng, N, 128, 512), **lists(rng)}
def setup_inputs_alike(rng):
    return {**setup_inputs(rng), **lists(rng, alike=True)}
def setup_inputs_pairs(rng):
    d = setup_inputs(rng)
    uni, need = np.full((N, 2, UN), -1), np.full((N, N, CR), -1)
    for g in range(2):
        mates = rng.permutation([r for r in range(N) if HOST[r] == g])
        for q in range(N):
            at = rng.permutation(UN)[:2 * CR]
            uni[q, g, at] = rng.permutation(T)[:2 * CR]
            for i, r in enumerate(mates):
                need[r, q] = rng.permutation(at[:CR] if i < len(mates) // 2 else at[CR:])
    pos = [table(rng.choice(N * CR, W)) for r in range(N)]
    return {**d, "uni": np.stack([table(e.reshape(-1)) for e in uni]), "need": np.stack([table(e.reshape(-1)) for e in need]), "pos": np.stack(pos)}
def setup_inputs_full(rng):
    return {**setup_inputs(rng), **lists(rng, full=True)}
def setup_inputs_few(rng):
    d = {**setup_inputs(rng), **lists(rng, full=True)}
    uni = np.stack([entries(e) for e in d["uni"]]).reshape(N, 2, UN)
    need = np.stack([entries(e) for e in d["need"]]).reshape(N, N, CR)
    pos = [None] * N
    for g in range(2):
        p = rng.permutation(N)
        h = [HOST[q] for q in p]
        lead = [h.index(0), h.index(1)]
        own = np.concatenate([p[lead], np.delete(p, lead)])[:-(-W // CR)]
        rest = np.setdiff1d(np.arange(N), own)
        uni[rest, g] = -1
        for r in range(N):
            if HOST[r] != g: continue
            need[r, rest] = -1
            s = rng.permutation(own)[:, None] * CR + np.arange(CR)
            s[-1] = rng.permutation(s[-1])
            pos[r] = table(rng.permutation(s.reshape(-1)[:W]))
    return {**d, "uni": np.stack([table(e.reshape(-1)) for e in uni]), "need": np.stack([table(e.reshape(-1)) for e in need]), "pos": np.stack(pos)}
def setup_inputs_spread(rng):
    d = setup_inputs(rng); d["c"] = wide(rng, N, 128, 4 * T, cols=6); return d
def check_inputs(d):
    b = []
    uni = np.stack([entries(e) for e in d["uni"]]).reshape(N, 2, UN)
    need = np.stack([entries(e) for e in d["need"]]).reshape(N, N, CR)
    if uni.min() < -1 or uni.max() >= T: b.append("uni")
    if need.min() < -1 or need.max() >= UN: return b + ["need"]
    for q in range(N):
        for g in range(2):
            e = uni[q, g][uni[q, g] >= 0]
            if len(set(e.tolist())) != len(e): b.append("a column of one owner twice for one host")
            named = set()
            for r in range(N):
                if HOST[r] != g: continue
                k = need[r, q][need[r, q] >= 0]
                if len(set(k.tolist())) != len(k): b.append("need names an entry of one union twice")
                if (uni[q, g][k] < 0).any(): b.append("need names an empty entry of uni")
                named |= set(k.tolist())
            if set(np.flatnonzero(uni[q, g] >= 0).tolist()) - named: b.append("an entry of uni that no rank of the host needs")
    for r in range(N):
        p = entries(d["pos"][r])
        if p.min() < 0 or p.max() >= N * CR or (need[r].reshape(-1)[p] < 0).any(): b.append("pos")
    return b
def reference(c, w, uni, need, pos):
    uni = np.stack([entries(e) for e in uni]).reshape(N, 2, UN)
    need = np.stack([entries(e) for e in need]).reshape(N, N, CR)
    y = np.zeros((N, 128, W), np.float32)
    for r in range(N):
        g = HOST[r]
        t = np.concatenate([cols(c[q], np.where(need[r, q] >= 0, uni[q, g][need[r, q]], -1)) for q in range(N)], axis=1)
        y[r] = mx_ref.matmul(mx_ref.quantize(w[r]), mx_ref.quantize(cols(t, entries(pos[r]))))
    return {"y": y}

@@ -1,0 +1,254 @@
+from concourse.bass import DstId, RemoteDMATransfer
+from concourse.mybir import dt, AluOpType, ActivationFunctionType
+
+N, UN, CR, T_COLS, W = 8, 160, 80, 512, 512
+PER = 4
+BLK = 2 * CR
+LU, LN = UN // 16, CR // 16
+
+SCRATCH = {
+    "needs": ("sbuf", [128, N, LN], "int32"),
+    "nlist": ("sbuf", [128, PER, 2 * LN], "uint16"),
+    "nown": ("sbuf", [128, 2 * LN], "uint16"),
+    "nland": ("sbuf", [128, 3 * 2 * LN], "uint16"),
+    "unis": ("sbuf", [128, 2 * LU], "int32"),
+    "uoff": ("sbuf", [128, 2 * LU], "uint16"),
+    "poss": ("sbuf", [128, W // 16], "int32"),
+    "pa": ("sbuf", [128, W // 16], "int32"),
+    "pb": ("sbuf", [128, W // 16], "int32"),
+    "b1": ("sbuf", [128, W // 16], "int32"),
+    "b2": ("sbuf", [128, W // 16], "int32"),
+    "b3": ("sbuf", [128, W // 16], "int32"),
+    "b4": ("sbuf", [128, W // 16], "int32"),
+    "s1": ("sbuf", [128, W // 16], "int32"),
+    "s2": ("sbuf", [128, W // 16], "int32"),
+    "s3": ("sbuf", [128, W // 16], "int32"),
+    "poff": ("sbuf", [128, W // 16], "uint16"),
+    "ct": ("sbuf", [128, 4 * T_COLS], "bfloat16"),
+    "wt": ("sbuf", [128, 512], "bfloat16"),
+    "cq": ("sbuf", [128, T_COLS], "float8_e4m3fn_x4"),
+    "cs": ("sbuf", [128, T_COLS], "uint8"),
+    "wq": ("sbuf", [128, 128], "float8_e4m3fn_x4"),
+    "ws": ("sbuf", [128, 128], "uint8"),
+    "xq": ("sbuf", [128, UN], "float8_e4m3fn_x4"),
+    "xs": ("sbuf", [128, UN], "uint8"),
+    "winq": ("sbuf", [128, 2 * UN], "float8_e4m3fn_x4"),
+    "wins": ("sbuf", [128, 2 * UN], "uint8"),
+    "vq": ("sbuf", [128, 3 * BLK], "float8_e4m3fn_x4"),
+    "vs": ("sbuf", [128, 3 * BLK], "uint8"),
+    "landq": ("sbuf", [128, PER * BLK], "float8_e4m3fn_x4"),
+    "lands": ("sbuf", [128, PER * BLK], "uint8"),
+    "hn": ("sbuf", [128, 2 * LN], "uint16"),
+    "hq": ("sbuf", [128, BLK], "float8_e4m3fn_x4"),
+    "hs": ("sbuf", [128, BLK], "uint8"),
+    "ps": ("psum", [128, 512 * PER], "float32"),
+    "res": ("sbuf", [128, PER * BLK], "float32"),
+    "yt": ("sbuf", [128, W], "float32"),
+}
+PEERS = ["near", "far", "par"]
+SEMAPHORES = (["ld_need", "ld_uni", "ld_c", "ld_w", "ld_pos", "sent",
+               "v_n0", "v_n1", "v_o0", "v_o1", "v_u", "v_qc", "v_qw", "v_xq", "a_xs", "v_wq", "a_ws",
+               "x_q", "x_s", "h_n", "h_q", "h_s",
+               "v_p0", "v_p1", "v_p2", "v_p3", "v_p4", "v_p5", "v_p6", "v_p7", "v_p8", "v_p9", "v_po",
+               "v_op", "a_op", "v_sp", "a_sp", "v_me", "a_me", "v_y", "a_y", "st0", "st1"]
+              + ["n_" + p for p in PEERS] + ["q_" + p for p in PEERS] + ["s_" + p for p in PEERS]
+              + ["mm%d" % b for b in range(4)] + ["cp%d" % b for b in range(4)])
+
+
+def mask_of(engines):
+    return sum(1 << e for e in engines)
+
+
+def plan(T, topo, r):
+    me = T.cores[r]
+    mates = [q for q in range(N) if topo.host(T.cores[q]) == topo.host(me) and q != r]
+    par = [q for q in mates if topo.may_write(me, T.cores[q])][0]
+    near = r ^ 1
+    far = [q for q in mates if q not in (par, near)][0]
+    own = [c for c in topo.cores_of(me) if c != me]
+    hnear = [c for c in own if topo.may_write(c, T.cores[near]) and topo.die(c) == topo.die(me)][0]
+    hfar = [c for c in own if topo.may_write(c, T.cores[far]) and topo.die(c) != topo.die(me)][0]
+    return {"near": near, "far": far, "par": par, "hnear": hnear, "hfar": hfar}
+
+
+def helper_program(g, core, T, topo, r, role, pl):
+    d = pl[role]
+    dst = T.cores[d]
+    rid, pid = topo.addr(dst, core)
+    m = mask_of(topo.engines(core, dst)[:8])
+    slot = PEERS.index(role)
+    b = (r % PER) * BLK
+    S = T.sem
+    g.wait_ge(S.h_n, 4)
+    g.remote_dma(T.nland[:, slot * 2 * LN:(slot + 1) * 2 * LN], T.hn[:], S["n_" + role], S.sent, pid, rid, m)
+    g.wait_ge(S.h_q, 8)
+    g.remote_dma(T.landq[:, b:b + BLK].bitcast(dt.uint8), T.hq[:, 0:BLK].bitcast(dt.uint8), S["q_" + role], S.sent, pid, rid, m)
+    g.wait_ge(S.h_s, 8)
+    g.remote_dma(T.lands[:, b:b + BLK], T.hs[:, 0:BLK], S["s_" + role], S.sent, pid, rid, m)
+    g.wait_ge(S.sent, 24)
+
+
+def rank_program(g, core, T, topo):
+    r = T.rank_of(core)
+    if r is None:
+        for q in range(N):
+            if core in topo.cores_of(T.cores[q]):
+                pl = plan(T, topo, q)
+                for role in ("near", "far"):
+                    if core == pl["h" + role]:
+                        helper_program(g, core, T, topo, q, role, pl)
+        return
+    S = T.sem
+    v, a, te, sy = g.vector, g.scalar, g.tensor, g.sync
+    COPY = ActivationFunctionType.Copy
+    pl = plan(T, topo, r)
+    h, b = r // PER, r % PER
+    own0, oth0 = h * UN, (1 - h) * UN
+    xh = T.cores[(r + PER) % N]
+
+    a.dma_start(T.ct[:], T.c[:]).then_inc(S.ld_c, 16)
+    for i in range(8):
+        (sy if i % 2 == 0 else a).dma_start(T.needs[16 * i:16 * i + 16, :, :], T.need[:]).then_inc(S.ld_need, 16)
+    for i in range(8):
+        (sy if i % 2 == 0 else a).dma_start(T.unis[16 * i:16 * i + 16, :], T.uni[:]).then_inc(S.ld_uni, 16)
+    sy.dma_start(T.wt[:], T.w[:]).then_inc(S.ld_w, 16)
+    for i in range(8):
+        sy.dma_start(T.poss[16 * i:16 * i + 16, :], T.pos[:]).then_inc(S.ld_pos, 16)
+
+    v.wait_ge(S.ld_need, 128)
+    v.tensor_copy(T.nlist[:, :, 0:LN], T.needs[:, 0:PER, :]).then_inc(S.v_n0, 1)
+    v.tensor_scalar(T.nlist[:, :, LN:2 * LN], T.needs[:, PER:N, :], float(UN), None, AluOpType.add).then_inc(S.v_n1, 1)
+    v.wait_ge(S.ld_uni, 128)
+    v.tensor_copy(T.uoff[:], T.unis[:]).then_inc(S.v_u, 1)
+    v.wait_ge(S.ld_c, 16)
+    v.quantize_mx(T.cq[:, 0:T_COLS], T.cs[:, 0:T_COLS], T.ct[:, 0:4 * T_COLS]).then_inc(S.v_qc, 1)
+    uoth, uown = T.uoff[:, (1 - h) * LU:(2 - h) * LU], T.uoff[:, h * LU:(h + 1) * LU]
+    v.wait_ge(S.v_u, 1)
+    v.wait_ge(S.v_qc, 1)
+    v.tensor_copy(T.xq[:, 0:UN].bitcast(dt.uint32), T.cq[:, 0:T_COLS].bitcast(dt.uint32).indirect(uoth)).then_inc(S.v_xq, 1)
+    v.tensor_copy(T.winq[:, own0:own0 + UN].bitcast(dt.uint32), T.cq[:, 0:T_COLS].bitcast(dt.uint32).indirect(uown)).then_inc(S.v_wq, 1)
+    v.tensor_copy(T.nown[:, 0:LN], T.needs[:, b, :]).then_inc(S.v_o0, 1)
+    v.tensor_scalar(T.nown[:, LN:2 * LN], T.needs[:, PER + b, :], float(UN), None, AluOpType.add).then_inc(S.v_o1, 1)
+    v.wait_ge(S.ld_w, 16)
+    v.quantize_mx(T.wq[:, 0:128], T.ws[:, 0:128], T.wt[:, 0:512]).then_inc(S.v_qw, 1)
+    GE, MUL, ADD = AluOpType.is_ge, AluOpType.mult, AluOpType.add
+    v.wait_ge(S.ld_pos, 128)
+    v.tensor_scalar(T.pa[:], T.poss[:], float(PER * CR), float(PER * CR), GE, MUL).then_inc(S.v_p0, 1)
+    v.tensor_scalar(T.b4[:], T.poss[:], float(PER * CR), float(CR), GE, MUL).then_inc(S.v_p1, 1)
+    v.wait_ge(S.v_p0, 1)
+    v.tensor_tensor(T.pb[:], T.poss[:], T.pa[:], AluOpType.subtract).then_inc(S.v_p2, 1)
+    v.wait_ge(S.v_p2, 1)
+    v.tensor_scalar(T.b1[:], T.pb[:], float(CR), float(CR), GE, MUL).then_inc(S.v_p3, 1)
+    v.tensor_scalar(T.b2[:], T.pb[:], float(2 * CR), float(CR), GE, MUL).then_inc(S.v_p4, 1)
+    v.tensor_scalar(T.b3[:], T.pb[:], float(3 * CR), float(CR), GE, MUL).then_inc(S.v_p5, 1)
+    v.wait_ge(S.v_p3, 1)
+    v.wait_ge(S.v_p4, 1)
+    v.tensor_tensor(T.s1[:], T.b1[:], T.b2[:], ADD).then_inc(S.v_p6, 1)
+    v.wait_ge(S.v_p1, 1)
+    v.wait_ge(S.v_p5, 1)
+    v.tensor_tensor(T.s2[:], T.b3[:], T.b4[:], ADD).then_inc(S.v_p7, 1)
+    v.wait_ge(S.v_p6, 1)
+    v.wait_ge(S.v_p7, 1)
+    v.tensor_tensor(T.s3[:], T.s1[:], T.s2[:], ADD).then_inc(S.v_p8, 1)
+    v.wait_ge(S.v_p8, 1)
+    v.tensor_tensor(T.pa[:], T.s3[:], T.pb[:], ADD).then_inc(S.v_p9, 1)
+    v.wait_ge(S.v_p9, 1)
+    v.tensor_copy(T.poff[:], T.pa[:]).then_inc(S.v_po, 1)
+    K = 2 * LN
+    wq_, ws_ = T.winq[:, 0:2 * UN], T.wins[:, 0:2 * UN]
+    v.wait_ge(S.v_wq, 1)
+    v.wait_ge(S.n_near, 8)
+    v.wait_ge(S.n_far, 8)
+    v.wait_ge(S.x_q, 8)
+    v.tensor_copy(T.vq[:, 0:2 * BLK].bitcast(dt.uint32), wq_.bitcast(dt.uint32).indirect(T.nland[:, 0:2 * K])).then_inc(S.v_op, 1)
+    v.wait_ge(S.n_par, 8)
+    v.tensor_copy(T.vq[:, 2 * BLK:3 * BLK].bitcast(dt.uint32), wq_.bitcast(dt.uint32).indirect(T.nland[:, 2 * K:3 * K])).then_inc(S.v_sp, 1)
+    v.wait_ge(S.v_o0, 1)
+    v.wait_ge(S.v_o1, 1)
+    v.tensor_copy(T.landq[:, b * BLK:(b + 1) * BLK].bitcast(dt.uint32), wq_.bitcast(dt.uint32).indirect(T.nown[:, 0:K])).then_inc(S.v_me, 1)
+
+    a.wait_ge(S.v_u, 1)
+    a.wait_ge(S.v_qc, 1)
+    a.activation(T.xs[:, 0:UN], T.cs[:, 0:T_COLS].indirect(uoth), COPY).then_inc(S.a_xs, 1)
+    a.activation(T.wins[:, own0:own0 + UN], T.cs[:, 0:T_COLS].indirect(uown), COPY).then_inc(S.a_ws, 1)
+    a.wait_ge(S.a_ws, 1)
+    a.wait_ge(S.n_near, 8)
+    a.wait_ge(S.n_far, 8)
+    a.wait_ge(S.x_s, 8)
+    a.activation(T.vs[:, 0:2 * BLK], ws_.indirect(T.nland[:, 0:2 * K]), COPY).then_inc(S.a_op, 1)
+    a.wait_ge(S.n_par, 8)
+    a.activation(T.vs[:, 2 * BLK:3 * BLK], ws_.indirect(T.nland[:, 2 * K:3 * K]), COPY).then_inc(S.a_sp, 1)
+    a.wait_ge(S.v_o0, 1)
+    a.wait_ge(S.v_o1, 1)
+    a.activation(T.lands[:, b * BLK:(b + 1) * BLK], ws_.indirect(T.nown[:, 0:K]), COPY).then_inc(S.a_me, 1)
+
+    def did(dst):
+        rid, pid = topo.addr(dst, core)
+        return [DstId(rid=rid, pnc=pid)]
+
+    hn, hf, sp = pl["hnear"], pl["hfar"], T.cores[pl["par"]]
+    en, ef = topo.engines(core, hn), topo.engines(core, hf)
+    mp, mx = mask_of(topo.engines(core, sp)[:8]), mask_of(topo.engines(core, xh)[:8])
+    half = len(en) // 2
+    nd, fd, pd = pl["near"] % PER, pl["far"] % PER, pl["par"] % PER
+    g.wait_ge(S.v_n0, 1)
+    g.wait_ge(S.v_n1, 1)
+    g.remote_dma_fused([
+        RemoteDMATransfer(dst_ids=did(hn), dma_engine_mask=mask_of(en[half:half + 4]), remote_sem=S.h_n, src=T.nlist[:, nd, :], dst=T.hn[:]),
+        RemoteDMATransfer(dst_ids=did(hf), dma_engine_mask=mask_of(ef[half + 4:half + 8]), remote_sem=S.h_n, src=T.nlist[:, fd, :], dst=T.hn[:]),
+    ], local_sem=S.sent)
+    rid, pid = topo.addr(sp, core)
+    g.remote_dma(T.nland[:, 2 * K:3 * K], T.nlist[:, pd, :], S.n_par, S.sent, pid, rid, mp)
+    xrid, xpid = topo.addr(xh, core)
+    xo = own0
+    g.wait_ge(S.v_xq, 1)
+    g.remote_dma(T.winq[:, xo:xo + UN].bitcast(dt.uint8), T.xq[:, 0:UN].bitcast(dt.uint8), S.x_q, S.sent, xpid, xrid, mx)
+    g.wait_ge(S.a_xs, 1)
+    g.remote_dma(T.wins[:, xo:xo + UN], T.xs[:, 0:UN], S.x_s, S.sent, xpid, xrid, mx)
+    g.wait_ge(S.v_op, 1)
+    g.remote_dma_fused([
+        RemoteDMATransfer(dst_ids=did(hn), dma_engine_mask=mask_of(en[:half]), remote_sem=S.h_q, src=T.vq[:, 0:BLK].bitcast(dt.uint8), dst=T.hq[:, 0:BLK].bitcast(dt.uint8)),
+        RemoteDMATransfer(dst_ids=did(hf), dma_engine_mask=mask_of(ef[half:]), remote_sem=S.h_q, src=T.vq[:, BLK:2 * BLK].bitcast(dt.uint8), dst=T.hq[:, 0:BLK].bitcast(dt.uint8)),
+    ], local_sem=S.sent)
+    g.wait_ge(S.a_op, 1)
+    g.remote_dma_fused([
+        RemoteDMATransfer(dst_ids=did(hn), dma_engine_mask=mask_of(en[:half]), remote_sem=S.h_s, src=T.vs[:, 0:BLK], dst=T.hs[:, 0:BLK]),
+        RemoteDMATransfer(dst_ids=did(hf), dma_engine_mask=mask_of(ef[half:]), remote_sem=S.h_s, src=T.vs[:, BLK:2 * BLK], dst=T.hs[:, 0:BLK]),
+    ], local_sem=S.sent)
+    g.wait_ge(S.v_sp, 1)
+    g.remote_dma(T.landq[:, b * BLK:(b + 1) * BLK].bitcast(dt.uint8), T.vq[:, 2 * BLK:3 * BLK].bitcast(dt.uint8), S.q_par, S.sent, pid, rid, mp)
+    g.wait_ge(S.a_sp, 1)
+    g.remote_dma(T.lands[:, b * BLK:(b + 1) * BLK], T.vs[:, 2 * BLK:3 * BLK], S.s_par, S.sent, pid, rid, mp)
+    g.wait_ge(S.sent, 80)
+
+    te.wait_ge(S.v_qw, 1)
+    order = [(b, None), (pd, "par"), (nd, "near"), (fd, "far")]
+    for j, role in order:
+        if role is None:
+            te.wait_ge(S.v_me, 1)
+            te.wait_ge(S.a_me, 1)
+        else:
+            te.wait_ge(S["q_" + role], 8)
+            te.wait_ge(S["s_" + role], 8)
+        te.matmul_mx(T.ps[:, 512 * j:512 * j + BLK], T.wq[:, 0:128], T.ws[:, 0:128],
+                     T.landq[:, j * BLK:(j + 1) * BLK], T.lands[:, j * BLK:(j + 1) * BLK], True, True).then_inc(S["mm%d" % j], 1)
+    for j in (b, nd):
+        v.wait_ge(S["mm%d" % j], 1)
+        v.tensor_copy(T.res[:, j * BLK:(j + 1) * BLK], T.ps[:, 512 * j:512 * j + BLK]).then_inc(S["cp%d" % j], 1)
+    for j in (pd, fd):
+        a.wait_ge(S["mm%d" % j], 1)
+        a.activation(T.res[:, j * BLK:(j + 1) * BLK], T.ps[:, 512 * j:512 * j + BLK], COPY).then_inc(S["cp%d" % j], 1)
+    for e in (v, a):
+        e.wait_ge(S.v_po, 1)
+        for j in range(PER):
+            e.wait_ge(S["cp%d" % j], 1)
+    win = T.res[:, 0:PER * BLK]
+    hw, hk = W // 2, W // 32
+    v.tensor_copy(T.yt[:, 0:hw], win.indirect(T.poff[:, 0:hk])).then_inc(S.v_y, 1)
+    a.activation(T.yt[:, hw:W], win.indirect(T.poff[:, hk:2 * hk]), COPY).then_inc(S.a_y, 1)
+    sy.wait_ge(S.v_y, 1)
+    sy.dma_start(T.y[:, 0:hw], T.yt[:, 0:hw]).then_inc(S.st0, 16)
+    sy.wait_ge(S.st0, 16)
+    a.wait_ge(S.a_y, 1)
+    a.dma_start(T.y[:, hw:W], T.yt[:, hw:W]).then_inc(S.st1, 16)
+    a.wait_ge(S.st1, 16)

@@ -5,46 +5,39 @@ N, UN, CR, T_COLS, W = 8, 160, 80, 512, 512
 PER = 4
 BLK = 2 * CR
 LU, LN = UN // 16, CR // 16
+CODES, I32, U16, F32 = "float8_e4m3fn_x4", "int32", "uint16", "float32"
 
 SCRATCH = {
-    "needs": ("sbuf", [128, N, LN], "int32"),
-    "nlist": ("sbuf", [128, PER, 2 * LN], "uint16"),
-    "nown": ("sbuf", [128, 2 * LN], "uint16"),
-    "nland": ("sbuf", [128, 3 * 2 * LN], "uint16"),
-    "unis": ("sbuf", [128, 2 * LU], "int32"),
-    "uoff": ("sbuf", [128, 2 * LU], "uint16"),
-    "poss": ("sbuf", [128, W // 16], "int32"),
-    "pa": ("sbuf", [128, W // 16], "int32"),
-    "pb": ("sbuf", [128, W // 16], "int32"),
-    "b1": ("sbuf", [128, W // 16], "int32"),
-    "b2": ("sbuf", [128, W // 16], "int32"),
-    "b3": ("sbuf", [128, W // 16], "int32"),
-    "b4": ("sbuf", [128, W // 16], "int32"),
-    "s1": ("sbuf", [128, W // 16], "int32"),
-    "s2": ("sbuf", [128, W // 16], "int32"),
-    "s3": ("sbuf", [128, W // 16], "int32"),
-    "poff": ("sbuf", [128, W // 16], "uint16"),
+    "needs": ("sbuf", [128, N, LN], I32),
+    "nlist": ("sbuf", [128, PER, 2 * LN], U16),
+    "nown": ("sbuf", [128, 2 * LN], U16),
+    "nland": ("sbuf", [128, 3 * 2 * LN], U16),
+    "unis": ("sbuf", [128, 2 * LU], I32),
+    "uoff": ("sbuf", [128, 2 * LU], U16),
+    "poff": ("sbuf", [128, W // 16], U16),
     "ct": ("sbuf", [128, 4 * T_COLS], "bfloat16"),
     "wt": ("sbuf", [128, 512], "bfloat16"),
-    "cq": ("sbuf", [128, T_COLS], "float8_e4m3fn_x4"),
+    "cq": ("sbuf", [128, T_COLS], CODES),
     "cs": ("sbuf", [128, T_COLS], "uint8"),
-    "wq": ("sbuf", [128, 128], "float8_e4m3fn_x4"),
+    "wq": ("sbuf", [128, 128], CODES),
     "ws": ("sbuf", [128, 128], "uint8"),
-    "xq": ("sbuf", [128, UN], "float8_e4m3fn_x4"),
+    "xq": ("sbuf", [128, UN], CODES),
     "xs": ("sbuf", [128, UN], "uint8"),
-    "winq": ("sbuf", [128, 2 * UN], "float8_e4m3fn_x4"),
+    "winq": ("sbuf", [128, 2 * UN], CODES),
     "wins": ("sbuf", [128, 2 * UN], "uint8"),
-    "vq": ("sbuf", [128, 3 * BLK], "float8_e4m3fn_x4"),
+    "vq": ("sbuf", [128, 3 * BLK], CODES),
     "vs": ("sbuf", [128, 3 * BLK], "uint8"),
-    "landq": ("sbuf", [128, PER * BLK], "float8_e4m3fn_x4"),
+    "landq": ("sbuf", [128, PER * BLK], CODES),
     "lands": ("sbuf", [128, PER * BLK], "uint8"),
-    "hn": ("sbuf", [128, 2 * LN], "uint16"),
-    "hq": ("sbuf", [128, BLK], "float8_e4m3fn_x4"),
+    "hn": ("sbuf", [128, 2 * LN], U16),
+    "hq": ("sbuf", [128, BLK], CODES),
     "hs": ("sbuf", [128, BLK], "uint8"),
-    "ps": ("psum", [128, 512 * PER], "float32"),
-    "res": ("sbuf", [128, PER * BLK], "float32"),
-    "yt": ("sbuf", [128, W], "float32"),
+    "ps": ("psum", [128, 512 * PER], F32),
+    "res": ("sbuf", [128, PER * BLK], F32),
+    "yt": ("sbuf", [128, W], F32),
 }
+for n_ in ("poss", "pa", "pb", "b1", "b2", "b3", "b4", "s1", "s2", "s3"):
+    SCRATCH[n_] = ("sbuf", [128, W // 16], I32)
 PEERS = ["near", "far", "par"]
 SEMAPHORES = (["ld_need", "ld_uni", "ld_c", "ld_w", "ld_pos", "sent",
                "v_n0", "v_n1", "v_o0", "v_o1", "v_u", "v_qc", "v_qw", "v_xq", "a_xs", "v_wq", "a_ws",
@@ -72,8 +65,7 @@ def plan(T, topo, r):
 
 
 def helper_program(g, core, T, topo, r, role, pl):
-    d = pl[role]
-    dst = T.cores[d]
+    dst = T.cores[pl[role]]
     rid, pid = topo.addr(dst, core)
     m = mask_of(topo.engines(core, dst)[:8])
     slot = PEERS.index(role)
@@ -103,12 +95,12 @@ def rank_program(g, core, T, topo):
     COPY = ActivationFunctionType.Copy
     pl = plan(T, topo, r)
     h, b = r // PER, r % PER
-    own0, oth0 = h * UN, (1 - h) * UN
+    own0 = h * UN
     xh = T.cores[(r + PER) % N]
 
-    a.dma_start(T.ct[:], T.c[:]).then_inc(S.ld_c, 16)
     for i in range(8):
         (sy if i % 2 == 0 else a).dma_start(T.needs[16 * i:16 * i + 16, :, :], T.need[:]).then_inc(S.ld_need, 16)
+    a.dma_start(T.ct[:], T.c[:]).then_inc(S.ld_c, 16)
     for i in range(8):
         (sy if i % 2 == 0 else a).dma_start(T.unis[16 * i:16 * i + 16, :], T.uni[:]).then_inc(S.ld_uni, 16)
     sy.dma_start(T.wt[:], T.w[:]).then_inc(S.ld_w, 16)
@@ -129,6 +121,18 @@ def rank_program(g, core, T, topo):
     v.tensor_copy(T.winq[:, own0:own0 + UN].bitcast(dt.uint32), T.cq[:, 0:T_COLS].bitcast(dt.uint32).indirect(uown)).then_inc(S.v_wq, 1)
     v.tensor_copy(T.nown[:, 0:LN], T.needs[:, b, :]).then_inc(S.v_o0, 1)
     v.tensor_scalar(T.nown[:, LN:2 * LN], T.needs[:, PER + b, :], float(UN), None, AluOpType.add).then_inc(S.v_o1, 1)
+    K = 2 * LN
+    wq_, ws_ = T.winq[:, 0:2 * UN], T.wins[:, 0:2 * UN]
+    v.wait_ge(S.v_wq, 1)
+    v.wait_ge(S.n_near, 8)
+    v.wait_ge(S.n_far, 8)
+    v.wait_ge(S.x_q, 8)
+    v.tensor_copy(T.vq[:, 0:2 * BLK].bitcast(dt.uint32), wq_.bitcast(dt.uint32).indirect(T.nland[:, 0:2 * K])).then_inc(S.v_op, 1)
+    v.wait_ge(S.n_par, 8)
+    v.tensor_copy(T.vq[:, 2 * BLK:3 * BLK].bitcast(dt.uint32), wq_.bitcast(dt.uint32).indirect(T.nland[:, 2 * K:3 * K])).then_inc(S.v_sp, 1)
+    v.wait_ge(S.v_o0, 1)
+    v.wait_ge(S.v_o1, 1)
+    v.tensor_copy(T.landq[:, b * BLK:(b + 1) * BLK].bitcast(dt.uint32), wq_.bitcast(dt.uint32).indirect(T.nown[:, 0:K])).then_inc(S.v_me, 1)
     v.wait_ge(S.ld_w, 16)
     v.quantize_mx(T.wq[:, 0:128], T.ws[:, 0:128], T.wt[:, 0:512]).then_inc(S.v_qw, 1)
     GE, MUL, ADD = AluOpType.is_ge, AluOpType.mult, AluOpType.add
@@ -154,18 +158,6 @@ def rank_program(g, core, T, topo):
     v.tensor_tensor(T.pa[:], T.s3[:], T.pb[:], ADD).then_inc(S.v_p9, 1)
     v.wait_ge(S.v_p9, 1)
     v.tensor_copy(T.poff[:], T.pa[:]).then_inc(S.v_po, 1)
-    K = 2 * LN
-    wq_, ws_ = T.winq[:, 0:2 * UN], T.wins[:, 0:2 * UN]
-    v.wait_ge(S.v_wq, 1)
-    v.wait_ge(S.n_near, 8)
-    v.wait_ge(S.n_far, 8)
-    v.wait_ge(S.x_q, 8)
-    v.tensor_copy(T.vq[:, 0:2 * BLK].bitcast(dt.uint32), wq_.bitcast(dt.uint32).indirect(T.nland[:, 0:2 * K])).then_inc(S.v_op, 1)
-    v.wait_ge(S.n_par, 8)
-    v.tensor_copy(T.vq[:, 2 * BLK:3 * BLK].bitcast(dt.uint32), wq_.bitcast(dt.uint32).indirect(T.nland[:, 2 * K:3 * K])).then_inc(S.v_sp, 1)
-    v.wait_ge(S.v_o0, 1)
-    v.wait_ge(S.v_o1, 1)
-    v.tensor_copy(T.landq[:, b * BLK:(b + 1) * BLK].bitcast(dt.uint32), wq_.bitcast(dt.uint32).indirect(T.nown[:, 0:K])).then_inc(S.v_me, 1)
 
     a.wait_ge(S.v_u, 1)
     a.wait_ge(S.v_qc, 1)
@@ -200,11 +192,10 @@ def rank_program(g, core, T, topo):
     rid, pid = topo.addr(sp, core)
     g.remote_dma(T.nland[:, 2 * K:3 * K], T.nlist[:, pd, :], S.n_par, S.sent, pid, rid, mp)
     xrid, xpid = topo.addr(xh, core)
-    xo = own0
     g.wait_ge(S.v_xq, 1)
-    g.remote_dma(T.winq[:, xo:xo + UN].bitcast(dt.uint8), T.xq[:, 0:UN].bitcast(dt.uint8), S.x_q, S.sent, xpid, xrid, mx)
+    g.remote_dma(T.winq[:, own0:own0 + UN].bitcast(dt.uint8), T.xq[:, 0:UN].bitcast(dt.uint8), S.x_q, S.sent, xpid, xrid, mx)
     g.wait_ge(S.a_xs, 1)
-    g.remote_dma(T.wins[:, xo:xo + UN], T.xs[:, 0:UN], S.x_s, S.sent, xpid, xrid, mx)
+    g.remote_dma(T.wins[:, own0:own0 + UN], T.xs[:, 0:UN], S.x_s, S.sent, xpid, xrid, mx)
     g.wait_ge(S.v_op, 1)
     g.remote_dma_fused([
         RemoteDMATransfer(dst_ids=did(hn), dma_engine_mask=mask_of(en[:half]), remote_sem=S.h_q, src=T.vq[:, 0:BLK].bitcast(dt.uint8), dst=T.hq[:, 0:BLK].bitcast(dt.uint8)),

@@ -5,13 +5,14 @@ N, UN, CR, T_COLS, W = 8, 160, 80, 512, 512
 PER = 4
 BLK = 2 * CR
 LU, LN = UN // 16, CR // 16
+K = 2 * LN
 CODES, I32, U16, F32 = "float8_e4m3fn_x4", "int32", "uint16", "float32"
 
 SCRATCH = {
     "needs": ("sbuf", [128, N, LN], I32),
-    "nlist": ("sbuf", [128, PER, 2 * LN], U16),
-    "nown": ("sbuf", [128, 2 * LN], U16),
-    "nland": ("sbuf", [128, 3 * 2 * LN], U16),
+    "nlist": ("sbuf", [128, PER, K], U16),
+    "nown": ("sbuf", [128, K], U16),
+    "nland": ("sbuf", [128, 3 * K], U16),
     "unis": ("sbuf", [128, 2 * LU], I32),
     "uoff": ("sbuf", [128, 2 * LU], U16),
     "poff": ("sbuf", [128, W // 16], U16),
@@ -29,7 +30,8 @@ SCRATCH = {
     "vs": ("sbuf", [128, 3 * BLK], "uint8"),
     "landq": ("sbuf", [128, PER * BLK], CODES),
     "lands": ("sbuf", [128, PER * BLK], "uint8"),
-    "hn": ("sbuf", [128, 2 * LN], U16),
+    "hn": ("sbuf", [128, K], U16),
+    "hp": ("sbuf", [128, LN], U16),
     "hq": ("sbuf", [128, BLK], CODES),
     "hs": ("sbuf", [128, BLK], "uint8"),
     "ps": ("psum", [128, 512 * PER], F32),
@@ -39,12 +41,12 @@ SCRATCH = {
 for n_ in ("poss", "pa", "pb", "b1", "b2", "b3", "b4", "s1", "s2", "s3"):
     SCRATCH[n_] = ("sbuf", [128, W // 16], I32)
 PEERS = ["near", "far", "par"]
-SEMAPHORES = (["ld_need", "ld_uni", "ld_c", "ld_w", "ld_pos", "sent",
+SEMAPHORES = (["ld_need", "ld_uni", "ld_c0", "ld_c1", "ld_w", "ld_pos", "sent",
                "v_n0", "v_n1", "v_o0", "v_o1", "v_u", "v_qc", "v_qw", "v_xq", "a_xs", "v_wq", "a_ws",
-               "x_q", "x_s", "h_n", "h_q", "h_s",
+               "x_q", "x_s", "h_n", "h_d",
                "v_p0", "v_p1", "v_p2", "v_p3", "v_p4", "v_p5", "v_p6", "v_p7", "v_p8", "v_p9", "v_po",
-               "v_op", "a_op", "v_sp", "a_sp", "v_me", "a_me", "v_y", "a_y", "st0", "st1"]
-              + ["n_" + p for p in PEERS] + ["q_" + p for p in PEERS] + ["s_" + p for p in PEERS]
+               "v_me", "a_me", "v_y0", "a_y0", "v_y1", "a_y1", "st0", "st1"]
+              + [x + p for x in ("n_", "q_", "s_", "v_", "a_") for p in PEERS]
               + ["mm%d" % b for b in range(4)] + ["cp%d" % b for b in range(4)])
 
 
@@ -59,25 +61,31 @@ def plan(T, topo, r):
     near = r ^ 1
     far = [q for q in mates if q not in (par, near)][0]
     own = [c for c in topo.cores_of(me) if c != me]
-    hnear = [c for c in own if topo.may_write(c, T.cores[near]) and topo.die(c) == topo.die(me)][0]
-    hfar = [c for c in own if topo.may_write(c, T.cores[far]) and topo.die(c) != topo.die(me)][0]
+    hnear = [c for c in own if topo.may_write(c, T.cores[near]) and topo.die(c) == topo.die(me)][:2]
+    hfar = [c for c in own if topo.may_write(c, T.cores[far]) and topo.die(c) != topo.die(me)][:2]
     return {"near": near, "far": far, "par": par, "hnear": hnear, "hfar": hfar}
 
 
 def helper_program(g, core, T, topo, r, role, pl):
-    dst = T.cores[pl[role]]
+    S = T.sem
+    dst, par = T.cores[pl[role]], T.cores[pl["par"]]
     rid, pid = topo.addr(dst, core)
     m = mask_of(topo.engines(core, dst)[:8])
-    slot = PEERS.index(role)
     b = (r % PER) * BLK
-    S = T.sem
-    g.wait_ge(S.h_n, 4)
-    g.remote_dma(T.nland[:, slot * 2 * LN:(slot + 1) * 2 * LN], T.hn[:], S["n_" + role], S.sent, pid, rid, m)
-    g.wait_ge(S.h_q, 8)
-    g.remote_dma(T.landq[:, b:b + BLK].bitcast(dt.uint8), T.hq[:, 0:BLK].bitcast(dt.uint8), S["q_" + role], S.sent, pid, rid, m)
-    g.wait_ge(S.h_s, 8)
-    g.remote_dma(T.lands[:, b:b + BLK], T.hs[:, 0:BLK], S["s_" + role], S.sent, pid, rid, m)
-    g.wait_ge(S.sent, 24)
+    slot = PEERS.index(role) * K
+    if core == pl["h" + role][0]:
+        g.wait_ge(S.h_n, 8)
+        g.remote_dma(T.nland[:, slot:slot + K], T.hn[:], S["n_" + role], S.sent, pid, rid, m)
+        g.wait_ge(S.h_d, 16)
+        g.remote_dma(T.landq[:, b:b + BLK].bitcast(dt.uint8), T.hq[:, 0:BLK].bitcast(dt.uint8), S["q_" + role], S.sent, pid, rid, m)
+    else:
+        prid, ppid = topo.addr(par, core)
+        e = 2 * K + (0 if role == "near" else LN)
+        g.wait_ge(S.h_n, 4)
+        g.remote_dma(T.nland[:, e:e + LN], T.hp[:], S.n_par, S.sent, ppid, prid, mask_of(topo.engines(core, par)[:8]))
+        g.wait_ge(S.h_d, 8)
+        g.remote_dma(T.lands[:, b:b + BLK], T.hs[:, 0:BLK], S["s_" + role], S.sent, pid, rid, m)
+    g.wait_ge(S.sent, 16)
 
 
 def rank_program(g, core, T, topo):
@@ -87,7 +95,7 @@ def rank_program(g, core, T, topo):
             if core in topo.cores_of(T.cores[q]):
                 pl = plan(T, topo, q)
                 for role in ("near", "far"):
-                    if core == pl["h" + role]:
+                    if core in pl["h" + role]:
                         helper_program(g, core, T, topo, q, role, pl)
         return
     S = T.sem
@@ -100,39 +108,60 @@ def rank_program(g, core, T, topo):
 
     for i in range(8):
         (sy if i % 2 == 0 else a).dma_start(T.needs[16 * i:16 * i + 16, :, :], T.need[:]).then_inc(S.ld_need, 16)
-    a.dma_start(T.ct[:], T.c[:]).then_inc(S.ld_c, 16)
+    for i in range(2):
+        a.dma_start(T.ct[:, 2 * T_COLS * i:2 * T_COLS * (i + 1)], T.c[:, 2 * T_COLS * i:2 * T_COLS * (i + 1)]).then_inc(S["ld_c%d" % i], 16)
     for i in range(8):
         (sy if i % 2 == 0 else a).dma_start(T.unis[16 * i:16 * i + 16, :], T.uni[:]).then_inc(S.ld_uni, 16)
+    sy.wait_ge(S.ld_need, 128)
     sy.dma_start(T.wt[:], T.w[:]).then_inc(S.ld_w, 16)
     for i in range(8):
         sy.dma_start(T.poss[16 * i:16 * i + 16, :], T.pos[:]).then_inc(S.ld_pos, 16)
 
+    def offs(who):
+        if who == "me":
+            return T.nown[:, 0:K]
+        e = PEERS.index(who) * K
+        return T.nland[:, e:e + K]
+
+    def place(who):
+        return (b if who == "me" else PEERS.index(who)) * BLK
+
+    def pick_codes(who):
+        p, out = place(who), T.landq if who == "me" else T.vq
+        v.tensor_copy(out[:, p:p + BLK].bitcast(dt.uint32), T.winq[:, 0:2 * UN].bitcast(dt.uint32).indirect(offs(who))).then_inc(S["v_" + who], 1)
+
+    def pick_scales(who):
+        p, out = place(who), T.lands if who == "me" else T.vs
+        a.activation(out[:, p:p + BLK], T.wins[:, 0:2 * UN].indirect(offs(who)), COPY).then_inc(S["a_" + who], 1)
+
     v.wait_ge(S.ld_need, 128)
     v.tensor_copy(T.nlist[:, :, 0:LN], T.needs[:, 0:PER, :]).then_inc(S.v_n0, 1)
-    v.tensor_scalar(T.nlist[:, :, LN:2 * LN], T.needs[:, PER:N, :], float(UN), None, AluOpType.add).then_inc(S.v_n1, 1)
+    v.tensor_scalar(T.nlist[:, :, LN:K], T.needs[:, PER:N, :], float(UN), None, AluOpType.add).then_inc(S.v_n1, 1)
+    hc = T_COLS // 2
+    v.wait_ge(S.ld_c0, 16)
+    v.quantize_mx(T.cq[:, 0:hc], T.cs[:, 0:hc], T.ct[:, 0:4 * hc]).then_inc(S.v_qc, 1)
     v.wait_ge(S.ld_uni, 128)
     v.tensor_copy(T.uoff[:], T.unis[:]).then_inc(S.v_u, 1)
-    v.wait_ge(S.ld_c, 16)
-    v.quantize_mx(T.cq[:, 0:T_COLS], T.cs[:, 0:T_COLS], T.ct[:, 0:4 * T_COLS]).then_inc(S.v_qc, 1)
+    v.wait_ge(S.ld_c1, 16)
+    v.quantize_mx(T.cq[:, hc:T_COLS], T.cs[:, hc:T_COLS], T.ct[:, 4 * hc:4 * T_COLS]).then_inc(S.v_qc, 1)
     uoth, uown = T.uoff[:, (1 - h) * LU:(2 - h) * LU], T.uoff[:, h * LU:(h + 1) * LU]
     v.wait_ge(S.v_u, 1)
-    v.wait_ge(S.v_qc, 1)
+    v.wait_ge(S.v_qc, 2)
     v.tensor_copy(T.xq[:, 0:UN].bitcast(dt.uint32), T.cq[:, 0:T_COLS].bitcast(dt.uint32).indirect(uoth)).then_inc(S.v_xq, 1)
     v.tensor_copy(T.winq[:, own0:own0 + UN].bitcast(dt.uint32), T.cq[:, 0:T_COLS].bitcast(dt.uint32).indirect(uown)).then_inc(S.v_wq, 1)
     v.tensor_copy(T.nown[:, 0:LN], T.needs[:, b, :]).then_inc(S.v_o0, 1)
-    v.tensor_scalar(T.nown[:, LN:2 * LN], T.needs[:, PER + b, :], float(UN), None, AluOpType.add).then_inc(S.v_o1, 1)
-    K = 2 * LN
-    wq_, ws_ = T.winq[:, 0:2 * UN], T.wins[:, 0:2 * UN]
+    v.tensor_scalar(T.nown[:, LN:K], T.needs[:, PER + b, :], float(UN), None, AluOpType.add).then_inc(S.v_o1, 1)
     v.wait_ge(S.v_wq, 1)
-    v.wait_ge(S.n_near, 8)
-    v.wait_ge(S.n_far, 8)
     v.wait_ge(S.x_q, 8)
-    v.tensor_copy(T.vq[:, 0:2 * BLK].bitcast(dt.uint32), wq_.bitcast(dt.uint32).indirect(T.nland[:, 0:2 * K])).then_inc(S.v_op, 1)
-    v.wait_ge(S.n_par, 8)
-    v.tensor_copy(T.vq[:, 2 * BLK:3 * BLK].bitcast(dt.uint32), wq_.bitcast(dt.uint32).indirect(T.nland[:, 2 * K:3 * K])).then_inc(S.v_sp, 1)
+    v.wait_ge(S.n_near, 8)
+    pick_codes("near")
+    v.wait_ge(S.n_far, 8)
+    pick_codes("far")
+    v.wait_ge(S.n_par, 16)
+    pick_codes("par")
     v.wait_ge(S.v_o0, 1)
     v.wait_ge(S.v_o1, 1)
-    v.tensor_copy(T.landq[:, b * BLK:(b + 1) * BLK].bitcast(dt.uint32), wq_.bitcast(dt.uint32).indirect(T.nown[:, 0:K])).then_inc(S.v_me, 1)
+    pick_codes("me")
     v.wait_ge(S.ld_w, 16)
     v.quantize_mx(T.wq[:, 0:128], T.ws[:, 0:128], T.wt[:, 0:512]).then_inc(S.v_qw, 1)
     GE, MUL, ADD = AluOpType.is_ge, AluOpType.mult, AluOpType.add
@@ -160,57 +189,61 @@ def rank_program(g, core, T, topo):
     v.tensor_copy(T.poff[:], T.pa[:]).then_inc(S.v_po, 1)
 
     a.wait_ge(S.v_u, 1)
-    a.wait_ge(S.v_qc, 1)
+    a.wait_ge(S.v_qc, 2)
     a.activation(T.xs[:, 0:UN], T.cs[:, 0:T_COLS].indirect(uoth), COPY).then_inc(S.a_xs, 1)
     a.activation(T.wins[:, own0:own0 + UN], T.cs[:, 0:T_COLS].indirect(uown), COPY).then_inc(S.a_ws, 1)
     a.wait_ge(S.a_ws, 1)
-    a.wait_ge(S.n_near, 8)
-    a.wait_ge(S.n_far, 8)
     a.wait_ge(S.x_s, 8)
-    a.activation(T.vs[:, 0:2 * BLK], ws_.indirect(T.nland[:, 0:2 * K]), COPY).then_inc(S.a_op, 1)
-    a.wait_ge(S.n_par, 8)
-    a.activation(T.vs[:, 2 * BLK:3 * BLK], ws_.indirect(T.nland[:, 2 * K:3 * K]), COPY).then_inc(S.a_sp, 1)
+    a.wait_ge(S.n_near, 8)
+    pick_scales("near")
+    a.wait_ge(S.n_far, 8)
+    pick_scales("far")
+    a.wait_ge(S.n_par, 16)
+    pick_scales("par")
     a.wait_ge(S.v_o0, 1)
     a.wait_ge(S.v_o1, 1)
-    a.activation(T.lands[:, b * BLK:(b + 1) * BLK], ws_.indirect(T.nown[:, 0:K]), COPY).then_inc(S.a_me, 1)
+    pick_scales("me")
 
     def did(dst):
         rid, pid = topo.addr(dst, core)
         return [DstId(rid=rid, pnc=pid)]
 
     hn, hf, sp = pl["hnear"], pl["hfar"], T.cores[pl["par"]]
-    en, ef = topo.engines(core, hn), topo.engines(core, hf)
+    en, ef = topo.engines(core, hn[0]), topo.engines(core, hf[0])
     mp, mx = mask_of(topo.engines(core, sp)[:8]), mask_of(topo.engines(core, xh)[:8])
     half = len(en) // 2
     nd, fd, pd = pl["near"] % PER, pl["far"] % PER, pl["par"] % PER
     g.wait_ge(S.v_n0, 1)
     g.wait_ge(S.v_n1, 1)
+    for d, hc_ in ((nd, hn[0]), (fd, hf[0])):
+        hrid, hpid = topo.addr(hc_, core)
+        g.remote_dma(T.hn[:], T.nlist[:, d, :], S.h_n, S.sent, hpid, hrid, mask_of(topo.engines(core, hc_)[half:]))
     g.remote_dma_fused([
-        RemoteDMATransfer(dst_ids=did(hn), dma_engine_mask=mask_of(en[half:half + 4]), remote_sem=S.h_n, src=T.nlist[:, nd, :], dst=T.hn[:]),
-        RemoteDMATransfer(dst_ids=did(hf), dma_engine_mask=mask_of(ef[half + 4:half + 8]), remote_sem=S.h_n, src=T.nlist[:, fd, :], dst=T.hn[:]),
+        RemoteDMATransfer(dst_ids=did(hn[1]), dma_engine_mask=mask_of(en[0:4]), remote_sem=S.h_n, src=T.nlist[:, pd, 0:LN], dst=T.hp[:]),
+        RemoteDMATransfer(dst_ids=did(hf[1]), dma_engine_mask=mask_of(ef[4:8]), remote_sem=S.h_n, src=T.nlist[:, pd, LN:K], dst=T.hp[:]),
     ], local_sem=S.sent)
-    rid, pid = topo.addr(sp, core)
-    g.remote_dma(T.nland[:, 2 * K:3 * K], T.nlist[:, pd, :], S.n_par, S.sent, pid, rid, mp)
     xrid, xpid = topo.addr(xh, core)
     g.wait_ge(S.v_xq, 1)
     g.remote_dma(T.winq[:, own0:own0 + UN].bitcast(dt.uint8), T.xq[:, 0:UN].bitcast(dt.uint8), S.x_q, S.sent, xpid, xrid, mx)
     g.wait_ge(S.a_xs, 1)
     g.remote_dma(T.wins[:, own0:own0 + UN], T.xs[:, 0:UN], S.x_s, S.sent, xpid, xrid, mx)
-    g.wait_ge(S.v_op, 1)
-    g.remote_dma_fused([
-        RemoteDMATransfer(dst_ids=did(hn), dma_engine_mask=mask_of(en[:half]), remote_sem=S.h_q, src=T.vq[:, 0:BLK].bitcast(dt.uint8), dst=T.hq[:, 0:BLK].bitcast(dt.uint8)),
-        RemoteDMATransfer(dst_ids=did(hf), dma_engine_mask=mask_of(ef[half:]), remote_sem=S.h_q, src=T.vq[:, BLK:2 * BLK].bitcast(dt.uint8), dst=T.hq[:, 0:BLK].bitcast(dt.uint8)),
-    ], local_sem=S.sent)
-    g.wait_ge(S.a_op, 1)
-    g.remote_dma_fused([
-        RemoteDMATransfer(dst_ids=did(hn), dma_engine_mask=mask_of(en[:half]), remote_sem=S.h_s, src=T.vs[:, 0:BLK], dst=T.hs[:, 0:BLK]),
-        RemoteDMATransfer(dst_ids=did(hf), dma_engine_mask=mask_of(ef[half:]), remote_sem=S.h_s, src=T.vs[:, BLK:2 * BLK], dst=T.hs[:, 0:BLK]),
-    ], local_sem=S.sent)
-    g.wait_ge(S.v_sp, 1)
+    to = {"far": (hf, ef[half:]), "near": (hn, en[:half])}
+    for who in ("near", "far"):
+        p, hc_ = place(who), to[who][0][0]
+        hrid, hpid = topo.addr(hc_, core)
+        g.wait_ge(S["v_" + who], 1)
+        g.remote_dma(T.hq[:, 0:BLK].bitcast(dt.uint8), T.vq[:, p:p + BLK].bitcast(dt.uint8), S.h_d, S.sent, hpid, hrid, mask_of(topo.engines(core, hc_)))
+    for who in ("near", "far"):
+        p, hs_ = place(who), to[who][0][1]
+        hrid, hpid = topo.addr(hs_, core)
+        g.wait_ge(S["a_" + who], 1)
+        g.remote_dma(T.hs[:, 0:BLK], T.vs[:, p:p + BLK], S.h_d, S.sent, hpid, hrid, mask_of(to[who][1]))
+    rid, pid = topo.addr(sp, core)
+    g.wait_ge(S.v_par, 1)
     g.remote_dma(T.landq[:, b * BLK:(b + 1) * BLK].bitcast(dt.uint8), T.vq[:, 2 * BLK:3 * BLK].bitcast(dt.uint8), S.q_par, S.sent, pid, rid, mp)
-    g.wait_ge(S.a_sp, 1)
+    g.wait_ge(S.a_par, 1)
     g.remote_dma(T.lands[:, b * BLK:(b + 1) * BLK], T.vs[:, 2 * BLK:3 * BLK], S.s_par, S.sent, pid, rid, mp)
-    g.wait_ge(S.sent, 80)
+    g.wait_ge(S.sent, 104)
 
     te.wait_ge(S.v_qw, 1)
     order = [(b, None), (pd, "par"), (nd, "near"), (fd, "far")]
@@ -223,10 +256,10 @@ def rank_program(g, core, T, topo):
             te.wait_ge(S["s_" + role], 8)
         te.matmul_mx(T.ps[:, 512 * j:512 * j + BLK], T.wq[:, 0:128], T.ws[:, 0:128],
                      T.landq[:, j * BLK:(j + 1) * BLK], T.lands[:, j * BLK:(j + 1) * BLK], True, True).then_inc(S["mm%d" % j], 1)
-    for j in (b, nd):
+    for j in (b, fd):
         v.wait_ge(S["mm%d" % j], 1)
         v.tensor_copy(T.res[:, j * BLK:(j + 1) * BLK], T.ps[:, 512 * j:512 * j + BLK]).then_inc(S["cp%d" % j], 1)
-    for j in (pd, fd):
+    for j in (pd, nd):
         a.wait_ge(S["mm%d" % j], 1)
         a.activation(T.res[:, j * BLK:(j + 1) * BLK], T.ps[:, 512 * j:512 * j + BLK], COPY).then_inc(S["cp%d" % j], 1)
     for e in (v, a):
@@ -234,12 +267,13 @@ def rank_program(g, core, T, topo):
         for j in range(PER):
             e.wait_ge(S["cp%d" % j], 1)
     win = T.res[:, 0:PER * BLK]
-    hw, hk = W // 2, W // 32
-    v.tensor_copy(T.yt[:, 0:hw], win.indirect(T.poff[:, 0:hk])).then_inc(S.v_y, 1)
-    a.activation(T.yt[:, hw:W], win.indirect(T.poff[:, hk:2 * hk]), COPY).then_inc(S.a_y, 1)
-    sy.wait_ge(S.v_y, 1)
-    sy.dma_start(T.y[:, 0:hw], T.yt[:, 0:hw]).then_inc(S.st0, 16)
-    sy.wait_ge(S.st0, 16)
-    a.wait_ge(S.a_y, 1)
-    a.dma_start(T.y[:, hw:W], T.yt[:, hw:W]).then_inc(S.st1, 16)
-    a.wait_ge(S.st1, 16)
+    qw, qk = W // 4, W // 64
+    for i in range(2):
+        c0, k0 = 2 * i * qw, 2 * i * qk
+        v.tensor_copy(T.yt[:, c0:c0 + qw], win.indirect(T.poff[:, k0:k0 + qk])).then_inc(S["v_y%d" % i], 1)
+        a.activation(T.yt[:, c0 + qw:c0 + 2 * qw], win.indirect(T.poff[:, k0 + qk:k0 + 2 * qk]), COPY).then_inc(S["a_y%d" % i], 1)
+        sy.wait_ge(S["v_y%d" % i], 1)
+        sy.wait_ge(S["a_y%d" % i], 1)
+        sy.dma_start(T.y[:, c0:c0 + 2 * qw], T.yt[:, c0:c0 + 2 * qw]).then_inc(S["st%d" % i], 16)
+    for i in range(2):
+        sy.wait_ge(S["st%d" % i], 16)

from concourse.bass import DstId, RemoteDMATransfer
from concourse.mybir import dt, AluOpType, ActivationFunctionType

N, UN, CR, T_COLS, W = 8, 160, 80, 512, 512
PER = 4
BLK = 2 * CR
LU, LN = UN // 16, CR // 16
K = 2 * LN
CODES, I32, U16, F32 = "float8_e4m3fn_x4", "int32", "uint16", "float32"

SCRATCH = {
    "needs": ("sbuf", [128, N, LN], I32),
    "nlist": ("sbuf", [128, PER, K], U16),
    "nown": ("sbuf", [128, K], U16),
    "nland": ("sbuf", [128, 3 * K], U16),
    "unis": ("sbuf", [128, 2 * LU], I32),
    "uoff": ("sbuf", [128, 2 * LU], U16),
    "poff": ("sbuf", [128, W // 16], U16),
    "ct": ("sbuf", [128, 4 * T_COLS], "bfloat16"),
    "wt": ("sbuf", [128, 512], "bfloat16"),
    "cq": ("sbuf", [128, T_COLS], CODES),
    "cs": ("sbuf", [128, T_COLS], "uint8"),
    "wq": ("sbuf", [128, 128], CODES),
    "ws": ("sbuf", [128, 128], "uint8"),
    "xq": ("sbuf", [128, UN], CODES),
    "xs": ("sbuf", [128, UN], "uint8"),
    "winq": ("sbuf", [128, 2 * UN], CODES),
    "wins": ("sbuf", [128, 2 * UN], "uint8"),
    "vq": ("sbuf", [128, 3 * BLK], CODES),
    "vs": ("sbuf", [128, 3 * BLK], "uint8"),
    "landq": ("sbuf", [128, PER * BLK], CODES),
    "lands": ("sbuf", [128, PER * BLK], "uint8"),
    "hn": ("sbuf", [128, K], U16),
    "hp": ("sbuf", [128, LN], U16),
    "hq": ("sbuf", [128, BLK], CODES),
    "hs": ("sbuf", [128, BLK], "uint8"),
    "ps": ("psum", [128, 512 * PER], F32),
    "res": ("sbuf", [128, PER * BLK], F32),
    "yt": ("sbuf", [128, W], F32),
}
for n_ in ("poss", "pa", "pb", "b1", "b2", "b3", "b4", "s1", "s2", "s3"):
    SCRATCH[n_] = ("sbuf", [128, W // 16], I32)
PEERS = ["near", "far", "par"]
SEMAPHORES = (["ld_need", "ld_uni", "ld_c0", "ld_c1", "ld_w", "ld_pos", "sent",
               "v_n0", "v_n1", "v_o0", "v_o1", "v_u", "v_qc", "v_qw", "v_xq", "a_xs", "v_wq", "a_ws",
               "x_q", "x_s", "h_n", "h_d",
               "v_p0", "v_p1", "v_p2", "v_p3", "v_p4", "v_p5", "v_p6", "v_p7", "v_p8", "v_p9", "v_po",
               "v_me", "a_me", "v_y0", "a_y0", "v_y1", "a_y1", "st0", "st1"]
              + [x + p for x in ("n_", "q_", "s_", "v_", "a_") for p in PEERS]
              + ["mm%d" % b for b in range(4)] + ["cp%d" % b for b in range(4)])


def mask_of(engines):
    return sum(1 << e for e in engines)


def plan(T, topo, r):
    me = T.cores[r]
    mates = [q for q in range(N) if topo.host(T.cores[q]) == topo.host(me) and q != r]
    par = [q for q in mates if topo.may_write(me, T.cores[q])][0]
    near = r ^ 1
    far = [q for q in mates if q not in (par, near)][0]
    own = [c for c in topo.cores_of(me) if c != me]
    hnear = [c for c in own if topo.may_write(c, T.cores[near]) and topo.die(c) == topo.die(me)][:2]
    hfar = [c for c in own if topo.may_write(c, T.cores[far]) and topo.die(c) != topo.die(me)][:2]
    return {"near": near, "far": far, "par": par, "hnear": hnear, "hfar": hfar}


def helper_program(g, core, T, topo, r, role, pl):
    S = T.sem
    dst, par = T.cores[pl[role]], T.cores[pl["par"]]
    rid, pid = topo.addr(dst, core)
    m = mask_of(topo.engines(core, dst)[:8])
    b = (r % PER) * BLK
    slot = PEERS.index(role) * K
    if core == pl["h" + role][0]:
        g.wait_ge(S.h_n, 8)
        g.remote_dma(T.nland[:, slot:slot + K], T.hn[:], S["n_" + role], S.sent, pid, rid, m)
        g.wait_ge(S.h_d, 16)
        g.remote_dma(T.landq[:, b:b + BLK].bitcast(dt.uint8), T.hq[:, 0:BLK].bitcast(dt.uint8), S["q_" + role], S.sent, pid, rid, m)
    else:
        prid, ppid = topo.addr(par, core)
        e = 2 * K + (0 if role == "near" else LN)
        g.wait_ge(S.h_n, 4)
        g.remote_dma(T.nland[:, e:e + LN], T.hp[:], S.n_par, S.sent, ppid, prid, mask_of(topo.engines(core, par)[:8]))
        g.wait_ge(S.h_d, 8)
        g.remote_dma(T.lands[:, b:b + BLK], T.hs[:, 0:BLK], S["s_" + role], S.sent, pid, rid, m)
    g.wait_ge(S.sent, 16)


def rank_program(g, core, T, topo):
    r = T.rank_of(core)
    if r is None:
        for q in range(N):
            if core in topo.cores_of(T.cores[q]):
                pl = plan(T, topo, q)
                for role in ("near", "far"):
                    if core in pl["h" + role]:
                        helper_program(g, core, T, topo, q, role, pl)
        return
    S = T.sem
    v, a, te, sy = g.vector, g.scalar, g.tensor, g.sync
    COPY = ActivationFunctionType.Copy
    pl = plan(T, topo, r)
    h, b = r // PER, r % PER
    own0 = h * UN
    xh = T.cores[(r + PER) % N]

    for i in range(8):
        (sy if i % 2 == 0 else a).dma_start(T.needs[16 * i:16 * i + 16, :, :], T.need[:]).then_inc(S.ld_need, 16)
    for i in range(2):
        a.dma_start(T.ct[:, 2 * T_COLS * i:2 * T_COLS * (i + 1)], T.c[:, 2 * T_COLS * i:2 * T_COLS * (i + 1)]).then_inc(S["ld_c%d" % i], 16)
    for i in range(8):
        (sy if i % 2 == 0 else a).dma_start(T.unis[16 * i:16 * i + 16, :], T.uni[:]).then_inc(S.ld_uni, 16)
    sy.wait_ge(S.ld_need, 128)
    sy.dma_start(T.wt[:], T.w[:]).then_inc(S.ld_w, 16)
    for i in range(8):
        sy.dma_start(T.poss[16 * i:16 * i + 16, :], T.pos[:]).then_inc(S.ld_pos, 16)

    def offs(who):
        if who == "me":
            return T.nown[:, 0:K]
        e = PEERS.index(who) * K
        return T.nland[:, e:e + K]

    def place(who):
        return (b if who == "me" else PEERS.index(who)) * BLK

    def pick_codes(who):
        p, out = place(who), T.landq if who == "me" else T.vq
        v.tensor_copy(out[:, p:p + BLK].bitcast(dt.uint32), T.winq[:, 0:2 * UN].bitcast(dt.uint32).indirect(offs(who))).then_inc(S["v_" + who], 1)

    def pick_scales(who):
        p, out = place(who), T.lands if who == "me" else T.vs
        a.activation(out[:, p:p + BLK], T.wins[:, 0:2 * UN].indirect(offs(who)), COPY).then_inc(S["a_" + who], 1)

    v.wait_ge(S.ld_need, 128)
    v.tensor_copy(T.nlist[:, :, 0:LN], T.needs[:, 0:PER, :]).then_inc(S.v_n0, 1)
    v.tensor_scalar(T.nlist[:, :, LN:K], T.needs[:, PER:N, :], float(UN), None, AluOpType.add).then_inc(S.v_n1, 1)
    hc = T_COLS // 2
    v.wait_ge(S.ld_c0, 16)
    v.quantize_mx(T.cq[:, 0:hc], T.cs[:, 0:hc], T.ct[:, 0:4 * hc]).then_inc(S.v_qc, 1)
    v.wait_ge(S.ld_uni, 128)
    v.tensor_copy(T.uoff[:], T.unis[:]).then_inc(S.v_u, 1)
    v.wait_ge(S.ld_c1, 16)
    v.quantize_mx(T.cq[:, hc:T_COLS], T.cs[:, hc:T_COLS], T.ct[:, 4 * hc:4 * T_COLS]).then_inc(S.v_qc, 1)
    uoth, uown = T.uoff[:, (1 - h) * LU:(2 - h) * LU], T.uoff[:, h * LU:(h + 1) * LU]
    v.wait_ge(S.v_u, 1)
    v.wait_ge(S.v_qc, 2)
    v.tensor_copy(T.xq[:, 0:UN].bitcast(dt.uint32), T.cq[:, 0:T_COLS].bitcast(dt.uint32).indirect(uoth)).then_inc(S.v_xq, 1)
    v.tensor_copy(T.winq[:, own0:own0 + UN].bitcast(dt.uint32), T.cq[:, 0:T_COLS].bitcast(dt.uint32).indirect(uown)).then_inc(S.v_wq, 1)
    v.tensor_copy(T.nown[:, 0:LN], T.needs[:, b, :]).then_inc(S.v_o0, 1)
    v.tensor_scalar(T.nown[:, LN:K], T.needs[:, PER + b, :], float(UN), None, AluOpType.add).then_inc(S.v_o1, 1)
    v.wait_ge(S.v_wq, 1)
    v.wait_ge(S.x_q, 8)
    v.wait_ge(S.n_near, 8)
    pick_codes("near")
    v.wait_ge(S.n_far, 8)
    pick_codes("far")
    v.wait_ge(S.n_par, 16)
    pick_codes("par")
    v.wait_ge(S.v_o0, 1)
    v.wait_ge(S.v_o1, 1)
    pick_codes("me")
    v.wait_ge(S.ld_w, 16)
    v.quantize_mx(T.wq[:, 0:128], T.ws[:, 0:128], T.wt[:, 0:512]).then_inc(S.v_qw, 1)
    GE, MUL, ADD = AluOpType.is_ge, AluOpType.mult, AluOpType.add
    v.wait_ge(S.ld_pos, 128)
    v.tensor_scalar(T.pa[:], T.poss[:], float(PER * CR), float(PER * CR), GE, MUL).then_inc(S.v_p0, 1)
    v.tensor_scalar(T.b4[:], T.poss[:], float(PER * CR), float(CR), GE, MUL).then_inc(S.v_p1, 1)
    v.wait_ge(S.v_p0, 1)
    v.tensor_tensor(T.pb[:], T.poss[:], T.pa[:], AluOpType.subtract).then_inc(S.v_p2, 1)
    v.wait_ge(S.v_p2, 1)
    v.tensor_scalar(T.b1[:], T.pb[:], float(CR), float(CR), GE, MUL).then_inc(S.v_p3, 1)
    v.tensor_scalar(T.b2[:], T.pb[:], float(2 * CR), float(CR), GE, MUL).then_inc(S.v_p4, 1)
    v.tensor_scalar(T.b3[:], T.pb[:], float(3 * CR), float(CR), GE, MUL).then_inc(S.v_p5, 1)
    v.wait_ge(S.v_p3, 1)
    v.wait_ge(S.v_p4, 1)
    v.tensor_tensor(T.s1[:], T.b1[:], T.b2[:], ADD).then_inc(S.v_p6, 1)
    v.wait_ge(S.v_p1, 1)
    v.wait_ge(S.v_p5, 1)
    v.tensor_tensor(T.s2[:], T.b3[:], T.b4[:], ADD).then_inc(S.v_p7, 1)
    v.wait_ge(S.v_p6, 1)
    v.wait_ge(S.v_p7, 1)
    v.tensor_tensor(T.s3[:], T.s1[:], T.s2[:], ADD).then_inc(S.v_p8, 1)
    v.wait_ge(S.v_p8, 1)
    v.tensor_tensor(T.pa[:], T.s3[:], T.pb[:], ADD).then_inc(S.v_p9, 1)
    v.wait_ge(S.v_p9, 1)
    v.tensor_copy(T.poff[:], T.pa[:]).then_inc(S.v_po, 1)

    a.wait_ge(S.v_u, 1)
    a.wait_ge(S.v_qc, 2)
    a.activation(T.xs[:, 0:UN], T.cs[:, 0:T_COLS].indirect(uoth), COPY).then_inc(S.a_xs, 1)
    a.activation(T.wins[:, own0:own0 + UN], T.cs[:, 0:T_COLS].indirect(uown), COPY).then_inc(S.a_ws, 1)
    a.wait_ge(S.a_ws, 1)
    a.wait_ge(S.x_s, 8)
    a.wait_ge(S.n_near, 8)
    pick_scales("near")
    a.wait_ge(S.n_far, 8)
    pick_scales("far")
    a.wait_ge(S.n_par, 16)
    pick_scales("par")
    a.wait_ge(S.v_o0, 1)
    a.wait_ge(S.v_o1, 1)
    pick_scales("me")

    def did(dst):
        rid, pid = topo.addr(dst, core)
        return [DstId(rid=rid, pnc=pid)]

    hn, hf, sp = pl["hnear"], pl["hfar"], T.cores[pl["par"]]
    en, ef = topo.engines(core, hn[0]), topo.engines(core, hf[0])
    mp, mx = mask_of(topo.engines(core, sp)[:8]), mask_of(topo.engines(core, xh)[:8])
    half = len(en) // 2
    nd, fd, pd = pl["near"] % PER, pl["far"] % PER, pl["par"] % PER
    g.wait_ge(S.v_n0, 1)
    g.wait_ge(S.v_n1, 1)
    for d, hc_ in ((nd, hn[0]), (fd, hf[0])):
        hrid, hpid = topo.addr(hc_, core)
        g.remote_dma(T.hn[:], T.nlist[:, d, :], S.h_n, S.sent, hpid, hrid, mask_of(topo.engines(core, hc_)[half:]))
    g.remote_dma_fused([
        RemoteDMATransfer(dst_ids=did(hn[1]), dma_engine_mask=mask_of(en[0:4]), remote_sem=S.h_n, src=T.nlist[:, pd, 0:LN], dst=T.hp[:]),
        RemoteDMATransfer(dst_ids=did(hf[1]), dma_engine_mask=mask_of(ef[4:8]), remote_sem=S.h_n, src=T.nlist[:, pd, LN:K], dst=T.hp[:]),
    ], local_sem=S.sent)
    xrid, xpid = topo.addr(xh, core)
    g.wait_ge(S.v_xq, 1)
    g.remote_dma(T.winq[:, own0:own0 + UN].bitcast(dt.uint8), T.xq[:, 0:UN].bitcast(dt.uint8), S.x_q, S.sent, xpid, xrid, mx)
    g.wait_ge(S.a_xs, 1)
    g.remote_dma(T.wins[:, own0:own0 + UN], T.xs[:, 0:UN], S.x_s, S.sent, xpid, xrid, mx)
    to = {"far": (hf, ef[half:]), "near": (hn, en[:half])}
    for who in ("near", "far"):
        p, hc_ = place(who), to[who][0][0]
        hrid, hpid = topo.addr(hc_, core)
        g.wait_ge(S["v_" + who], 1)
        g.remote_dma(T.hq[:, 0:BLK].bitcast(dt.uint8), T.vq[:, p:p + BLK].bitcast(dt.uint8), S.h_d, S.sent, hpid, hrid, mask_of(topo.engines(core, hc_)))
    for who in ("near", "far"):
        p, hs_ = place(who), to[who][0][1]
        hrid, hpid = topo.addr(hs_, core)
        g.wait_ge(S["a_" + who], 1)
        g.remote_dma(T.hs[:, 0:BLK], T.vs[:, p:p + BLK], S.h_d, S.sent, hpid, hrid, mask_of(to[who][1]))
    rid, pid = topo.addr(sp, core)
    g.wait_ge(S.v_par, 1)
    g.remote_dma(T.landq[:, b * BLK:(b + 1) * BLK].bitcast(dt.uint8), T.vq[:, 2 * BLK:3 * BLK].bitcast(dt.uint8), S.q_par, S.sent, pid, rid, mp)
    g.wait_ge(S.a_par, 1)
    g.remote_dma(T.lands[:, b * BLK:(b + 1) * BLK], T.vs[:, 2 * BLK:3 * BLK], S.s_par, S.sent, pid, rid, mp)
    g.wait_ge(S.sent, 104)

    te.wait_ge(S.v_qw, 1)
    order = [(b, None), (pd, "par"), (nd, "near"), (fd, "far")]
    for j, role in order:
        if role is None:
            te.wait_ge(S.v_me, 1)
            te.wait_ge(S.a_me, 1)
        else:
            te.wait_ge(S["q_" + role], 8)
            te.wait_ge(S["s_" + role], 8)
        te.matmul_mx(T.ps[:, 512 * j:512 * j + BLK], T.wq[:, 0:128], T.ws[:, 0:128],
                     T.landq[:, j * BLK:(j + 1) * BLK], T.lands[:, j * BLK:(j + 1) * BLK], True, True).then_inc(S["mm%d" % j], 1)
    for j in (b, fd):
        v.wait_ge(S["mm%d" % j], 1)
        v.tensor_copy(T.res[:, j * BLK:(j + 1) * BLK], T.ps[:, 512 * j:512 * j + BLK]).then_inc(S["cp%d" % j], 1)
    for j in (pd, nd):
        a.wait_ge(S["mm%d" % j], 1)
        a.activation(T.res[:, j * BLK:(j + 1) * BLK], T.ps[:, 512 * j:512 * j + BLK], COPY).then_inc(S["cp%d" % j], 1)
    for e in (v, a):
        e.wait_ge(S.v_po, 1)
        for j in range(PER):
            e.wait_ge(S["cp%d" % j], 1)
    win = T.res[:, 0:PER * BLK]
    qw, qk = W // 4, W // 64
    for i in range(2):
        c0, k0 = 2 * i * qw, 2 * i * qk
        v.tensor_copy(T.yt[:, c0:c0 + qw], win.indirect(T.poff[:, k0:k0 + qk])).then_inc(S["v_y%d" % i], 1)
        a.activation(T.yt[:, c0 + qw:c0 + 2 * qw], win.indirect(T.poff[:, k0 + qk:k0 + 2 * qk]), COPY).then_inc(S["a_y%d" % i], 1)
        sy.wait_ge(S["v_y%d" % i], 1)
        sy.wait_ge(S["a_y%d" % i], 1)
        sy.dma_start(T.y[:, c0:c0 + 2 * qw], T.yt[:, c0:c0 + 2 * qw]).then_inc(S["st%d" % i], 16)
    for i in range(2):
        sy.wait_ge(S["st%d" % i], 16)
